import numpy as np
import ml_dtypes


def mxq(x, axis, fmt="e4m3"):
    dtype, down = {"e4m3": (ml_dtypes.float8_e4m3fn, 7), "e5m2": (ml_dtypes.float8_e5m2, 14)}[fmt]
    v = np.moveaxis(np.asarray(x, np.float32).astype(ml_dtypes.bfloat16).astype(np.float64), axis, -1)
    blocks = v.reshape(v.shape[:-1] + (-1, 32))
    amax = np.abs(blocks).max(-1, keepdims=True)
    byte = np.maximum(np.where(amax > 0, np.frexp(amax)[1] - 1 + 127, 0) - down, 1)
    scale = np.exp2(byte - 127.0)
    codes = (blocks / scale).astype(np.float32).astype(dtype).astype(np.float64)
    return np.moveaxis((codes * scale).reshape(v.shape), -1, axis)


WIDE = False


def mx_kscale(k):
    if not WIDE:
        return np.ones(k)
    levels = np.array([10, -10, 5, -5, 0])
    if k % 512:
        return np.exp2(np.random.permutation(np.resize(levels, k // 32))).repeat(32)
    a = np.empty((k // 512, 16))
    for p in range(k // 512):
        a[p, :8] = np.random.permutation(np.resize(levels, 8))
        for g in range(8):
            far = levels[np.abs(levels - a[p, g]) >= 10]
            a[p, g + 8] = far[np.random.randint(len(far))]
    return np.exp2(a.ravel()).repeat(32)


def f64(x):
    return np.asarray(x).astype(np.float64)


def striped(idx):
    return np.tile(idx.reshape(-1, 16).T, (8, 1)).astype(np.uint16)


def unstriped(offs):
    return offs[:16].T.reshape(-1).astype(np.int64)


def relu(v):
    return np.maximum(v, 0.0)


def sigmoid(v):
    return 1.0 / (1.0 + np.exp(-np.maximum(v, -700.0)))


K, T, S, N = 512, 2048, 512, 256


def setup_inputs():
    n = np.random.standard_normal
    s = mx_kscale(K)[:, None]
    return {
        "xT": (n((K, T)) * s).astype(np.float32),
        "res": n((N, T)).astype(np.float32),
        "w1": (n((K, N)) / np.sqrt(K) / s).astype(np.float32),
        "w2": (n((K, N)) / np.sqrt(K) / s).astype(np.float32),
        "offs": striped(np.random.permutation(T)[:S]),
    }


def reference(xT, res, w1, w2, offs):
    r = f64(res)[:, unstriped(offs)]
    xq = mxq(f64(xT)[:, unstriped(offs)], 0, "e4m3")
    g = sigmoid(mxq(f64(w2), 0, "e4m3").T @ xq)
    y = relu(mxq(f64(w1), 0, "e4m3").T @ xq)
    return r + g * (y - r)

@@ -1,0 +1,128 @@
+from contextlib import ExitStack
+
+import concourse.mybir as mybir
+
+K, T, S, N = 512, 2048, 512, 256
+FLOPS = 2 * 2 * K * S * N
+
+F32 = mybir.dt.float32
+BF16 = mybir.dt.bfloat16
+U32 = mybir.dt.uint32
+U16 = mybir.dt.uint16
+U8 = mybir.dt.uint8
+FP8X4 = mybir.dt.float8_e4m3fn_x4
+ALU = mybir.AluOpType
+ACT = mybir.ActivationFunctionType
+
+P = 128
+PACK = 4
+HALF = S // 2
+LINE = 4
+
+
+def tile_picked_highway_relu_l_kernel(tc, xT, res, w1, w2, offs, out):
+    nc = tc.nc
+    m_tiles = N // P
+    with ExitStack() as ctx:
+        keep = ctx.enter_context(tc.tile_pool(name="keep", bufs=1))
+        psum = ctx.enter_context(tc.psum_pool(name="psum", bufs=1))
+
+        offsets = keep.tile([P, S // 16], U16, name="offsets")
+        x_rows = [keep.tile([P, T], F32, name=f"x_rows{t}") for t in range(PACK)]
+        w_raw = {name: keep.tile([P, PACK, N], F32, name=f"{name}_raw") for name in ("gate", "layer")}
+        res_rows = [keep.tile([P, T], F32, name=f"res_rows{m}") for m in range(m_tiles)]
+
+        x_by_slot = xT.rearrange("(p t) c -> t p c", t=PACK)
+        nc.sync.dma_start(x_rows[0][:], x_by_slot[0])
+        nc.sync.dma_start(offsets[:], offs)
+        for t in range(1, PACK):
+            nc.sync.dma_start(x_rows[t][:], x_by_slot[t])
+        nc.sync.dma_start(w_raw["gate"][:], w2.rearrange("(p t) n -> p t n", t=PACK))
+        nc.sync.dma_start(w_raw["layer"][:], w1.rearrange("(p t) n -> p t n", t=PACK))
+        for m in range(m_tiles):
+            nc.sync.dma_start(res_rows[m][:], res[m * P : (m + 1) * P, :])
+
+        warm = keep.tile([P, 2], F32, name="warm")
+        nc.vector.memset(warm[:, 0:1], 0.0)
+        nc.scalar.activation(warm[:, 1:2], warm[:, 0:1], ACT.Sigmoid)
+
+        half_offsets = [offsets[:, h * (HALF // 16) : (h + 1) * (HALF // 16)] for h in range(2)]
+
+        x_grouped = [keep.tile([P, HALF, PACK], BF16, name=f"x_grouped{h}", align_bytes=64) for h in range(2)]
+        for t in range(PACK):
+            for h in range(2):
+                nc.vector.tensor_copy(x_grouped[h][:, :, t], x_rows[t][:].indirect(half_offsets[h]))
+
+        def quantize(name, grouped, width):
+            codes = keep.tile([P, width], U32, name=f"{name}_codes", align_bytes=64)
+            scales = keep.tile([P, width], U8, name=f"{name}_scales", align_bytes=64)
+            nc.vector.quantize_mx(
+                out=codes[:].bitcast(FP8X4), scales=scales[:], in_=grouped[:].rearrange("p c t -> p (c t)")
+            )
+            return codes, scales
+
+        x_mx = [quantize(f"x{h}", x_grouped[h], HALF) for h in range(2)]
+
+        def group_weights(name, m, copy):
+            grouped = keep.tile([P, P, PACK], BF16, name=f"{name}_grouped{m}", align_bytes=64)
+            copy(
+                grouped[:].rearrange("p (c i) t -> p c t i", i=LINE),
+                w_raw[name][:, :, m * P : (m + 1) * P].rearrange("p t (c i) -> p c t i", i=LINE),
+            )
+            return grouped
+
+        def product(name, m, grouped):
+            codes, scales = quantize(f"{name}{m}", grouped, P)
+            acc = psum.tile([P, S], F32, name=f"{name}_acc{m}")
+            for h in range(2):
+                nc.tensor.matmul_mx(
+                    out=acc[:, h * HALF : (h + 1) * HALF],
+                    lhsT=codes[:].bitcast(FP8X4),
+                    lhsT_scale=scales[:],
+                    rhs=x_mx[h][0][:].bitcast(FP8X4),
+                    rhs_scale=x_mx[h][1][:],
+                    start=True,
+                    stop=True,
+                )
+            return acc
+
+        grouped = {}
+        grouped["gate", 0] = group_weights("gate", 0, nc.scalar.copy)
+        grouped["gate", 1] = group_weights("gate", 1, nc.scalar.copy)
+        grouped["layer", 0] = group_weights("layer", 0, nc.scalar.copy)
+        grouped["layer", 1] = group_weights("layer", 1, nc.vector.tensor_copy)
+        acc = {}
+        for name in ("gate", "layer"):
+            for m in range(m_tiles):
+                acc[name, m] = product(name, m, grouped[name, m])
+
+        take, carry, taken = {}, {}, {}
+        for m in range(m_tiles):
+            take[m] = keep.tile([P, S], F32, name=f"take{m}")
+            carry[m] = keep.tile([P, S], F32, name=f"carry{m}", tag=f"carry{m}")
+            nc.scalar.activation(take[m][:], acc["gate", m][:], ACT.Sigmoid)
+            nc.scalar.activation(carry[m][:], acc["gate", m][:], ACT.Sigmoid, scale=-1.0)
+
+        def layer_share(m, tag):
+            taken[m] = keep.tile([P, S], F32, name=f"taken{m}", tag=tag)
+            nc.vector.scalar_tensor_tensor(taken[m][:], acc["layer", m][:], 0.0, take[m][:], ALU.max, ALU.mult)
+
+        def res_share(m, first, width):
+            carried = keep.tile([P, width], F32, name=f"carried{m}_{first}")
+            picked = res_rows[m][:].indirect(offsets[:, first // 16 : (first + width) // 16])
+            nc.vector.tensor_tensor(carried[:], picked, carry[m][:, first : first + width], ALU.mult)
+            return carried
+
+        def finish(m, first, width, carried):
+            cols = slice(first, first + width)
+            result = keep.tile([P, width], F32, name=f"result{m}_{first}")
+            nc.vector.tensor_tensor(result[:], carried[:], taken[m][:, cols], ALU.add)
+            nc.sync.dma_start(out[m * P : (m + 1) * P, cols], result[:])
+
+        layer_share(0, "taken0")
+        carried = res_share(0, 0, S)
+        layer_share(1, "carry0")
+        finish(0, 0, S, carried)
+        halves = [res_share(1, h * HALF, HALF) for h in range(2)]
+        for h in range(2):
+            finish(1, h * HALF, HALF, halves[h])

@@ -1,6 +1,7 @@
 from contextlib import ExitStack
 
 import concourse.mybir as mybir
+from concourse.masks import make_identity
 
 K, T, S, N = 512, 2048, 512, 256
 FLOPS = 2 * 2 * K * S * N
@@ -45,6 +46,9 @@ def tile_picked_highway_relu_l_kernel(tc, xT, res, w1, w2, offs, out):
         warm = keep.tile([P, 2], F32, name="warm")
         nc.vector.memset(warm[:, 0:1], 0.0)
         nc.scalar.activation(warm[:, 1:2], warm[:, 0:1], ACT.Sigmoid)
+
+        identity = keep.tile([P, P], F32, name="identity")
+        make_identity(nc, identity[:])
 
         half_offsets = [offsets[:, h * (HALF // 16) : (h + 1) * (HALF // 16)] for h in range(2)]
 
@@ -119,10 +123,29 @@ def tile_picked_highway_relu_l_kernel(tc, xT, res, w1, w2, offs, out):
             nc.vector.tensor_tensor(result[:], carried[:], taken[m][:, cols], ALU.add)
             nc.sync.dma_start(out[m * P : (m + 1) * P, cols], result[:])
 
+        def finish_on_tensor(m, first, width, carried):
+            blocks = width // P
+            turned = psum.tile([P, blocks, P], F32, name=f"turned{first}")
+            for b in range(blocks):
+                cols = slice(first + b * P, first + (b + 1) * P)
+                nc.tensor.matmul(turned[:, b, :], taken[m][:, cols], identity[:], start=True, stop=False, is_transpose=True)
+                nc.tensor.matmul(
+                    turned[:, b, :], carried[:, b * P : (b + 1) * P], identity[:], start=False, stop=True, is_transpose=True
+                )
+            turned_sb = keep.tile([P, blocks, P], F32, name=f"turned_sb{first}")
+            nc.scalar.copy(turned_sb[:], turned[:])
+            back = psum.tile([P, blocks, P], F32, name=f"back{first}")
+            for b in range(blocks):
+                nc.tensor.transpose(back[:, b, :], turned_sb[:, b, :], identity[:])
+            result = keep.tile([P, width], F32, name=f"result{m}_{first}")
+            nc.scalar.copy(result[:], back[:].rearrange("p b c -> p (b c)"))
+            nc.scalar.dma_start(out[m * P : (m + 1) * P, first : first + width], result[:])
+
         layer_share(0, "taken0")
-        carried = res_share(0, 0, S)
+        halves = [res_share(0, h * HALF, HALF) for h in range(2)]
         layer_share(1, "carry0")
-        finish(0, 0, S, carried)
+        for h in range(2):
+            finish_on_tensor(0, h * HALF, HALF, halves[h])
         halves = [res_share(1, h * HALF, HALF) for h in range(2)]
         for h in range(2):
             finish(1, h * HALF, HALF, halves[h])

from contextlib import ExitStack

import concourse.mybir as mybir
from concourse.masks import make_identity

K, T, S, N = 512, 2048, 512, 256
FLOPS = 2 * 2 * K * S * N

F32 = mybir.dt.float32
BF16 = mybir.dt.bfloat16
U32 = mybir.dt.uint32
U16 = mybir.dt.uint16
U8 = mybir.dt.uint8
FP8X4 = mybir.dt.float8_e4m3fn_x4
ALU = mybir.AluOpType
ACT = mybir.ActivationFunctionType

P = 128
PACK = 4
HALF = S // 2
LINE = 4


def tile_picked_highway_relu_l_kernel(tc, xT, res, w1, w2, offs, out):
    nc = tc.nc
    m_tiles = N // P
    with ExitStack() as ctx:
        keep = ctx.enter_context(tc.tile_pool(name="keep", bufs=1))
        psum = ctx.enter_context(tc.psum_pool(name="psum", bufs=1))

        offsets = keep.tile([P, S // 16], U16, name="offsets")
        x_rows = [keep.tile([P, T], F32, name=f"x_rows{t}") for t in range(PACK)]
        w_raw = {name: keep.tile([P, PACK, N], F32, name=f"{name}_raw") for name in ("gate", "layer")}
        res_rows = [keep.tile([P, T], F32, name=f"res_rows{m}") for m in range(m_tiles)]

        x_by_slot = xT.rearrange("(p t) c -> t p c", t=PACK)
        nc.sync.dma_start(x_rows[0][:], x_by_slot[0])
        nc.sync.dma_start(offsets[:], offs)
        for t in range(1, PACK):
            nc.sync.dma_start(x_rows[t][:], x_by_slot[t])
        nc.sync.dma_start(w_raw["gate"][:], w2.rearrange("(p t) n -> p t n", t=PACK))
        nc.sync.dma_start(w_raw["layer"][:], w1.rearrange("(p t) n -> p t n", t=PACK))
        for m in range(m_tiles):
            nc.sync.dma_start(res_rows[m][:], res[m * P : (m + 1) * P, :])

        warm = keep.tile([P, 2], F32, name="warm")
        nc.vector.memset(warm[:, 0:1], 0.0)
        nc.scalar.activation(warm[:, 1:2], warm[:, 0:1], ACT.Sigmoid)

        identity = keep.tile([P, P], F32, name="identity")
        make_identity(nc, identity[:])

        half_offsets = [offsets[:, h * (HALF // 16) : (h + 1) * (HALF // 16)] for h in range(2)]

        x_grouped = [keep.tile([P, HALF, PACK], BF16, name=f"x_grouped{h}", align_bytes=64) for h in range(2)]
        for t in range(PACK):
            for h in range(2):
                nc.vector.tensor_copy(x_grouped[h][:, :, t], x_rows[t][:].indirect(half_offsets[h]))

        def quantize(name, grouped, width):
            codes = keep.tile([P, width], U32, name=f"{name}_codes", align_bytes=64)
            scales = keep.tile([P, width], U8, name=f"{name}_scales", align_bytes=64)
            nc.vector.quantize_mx(
                out=codes[:].bitcast(FP8X4), scales=scales[:], in_=grouped[:].rearrange("p c t -> p (c t)")
            )
            return codes, scales

        x_mx = [quantize(f"x{h}", x_grouped[h], HALF) for h in range(2)]

        def group_weights(name, m, copy):
            grouped = keep.tile([P, P, PACK], BF16, name=f"{name}_grouped{m}", align_bytes=64)
            copy(
                grouped[:].rearrange("p (c i) t -> p c t i", i=LINE),
                w_raw[name][:, :, m * P : (m + 1) * P].rearrange("p t (c i) -> p c t i", i=LINE),
            )
            return grouped

        def product(name, m, grouped):
            codes, scales = quantize(f"{name}{m}", grouped, P)
            acc = psum.tile([P, S], F32, name=f"{name}_acc{m}")
            for h in range(2):
                nc.tensor.matmul_mx(
                    out=acc[:, h * HALF : (h + 1) * HALF],
                    lhsT=codes[:].bitcast(FP8X4),
                    lhsT_scale=scales[:],
                    rhs=x_mx[h][0][:].bitcast(FP8X4),
                    rhs_scale=x_mx[h][1][:],
                    start=True,
                    stop=True,
                )
            return acc

        grouped = {}
        grouped["gate", 0] = group_weights("gate", 0, nc.scalar.copy)
        grouped["gate", 1] = group_weights("gate", 1, nc.scalar.copy)
        grouped["layer", 0] = group_weights("layer", 0, nc.scalar.copy)
        grouped["layer", 1] = group_weights("layer", 1, nc.vector.tensor_copy)
        acc = {}
        for name in ("gate", "layer"):
            for m in range(m_tiles):
                acc[name, m] = product(name, m, grouped[name, m])

        take, carry, taken = {}, {}, {}
        for m in range(m_tiles):
            take[m] = keep.tile([P, S], F32, name=f"take{m}")
            carry[m] = keep.tile([P, S], F32, name=f"carry{m}", tag=f"carry{m}")
            nc.scalar.activation(take[m][:], acc["gate", m][:], ACT.Sigmoid)
            nc.scalar.activation(carry[m][:], acc["gate", m][:], ACT.Sigmoid, scale=-1.0)

        def layer_share(m, tag):
            taken[m] = keep.tile([P, S], F32, name=f"taken{m}", tag=tag)
            nc.vector.scalar_tensor_tensor(taken[m][:], acc["layer", m][:], 0.0, take[m][:], ALU.max, ALU.mult)

        def res_share(m, first, width):
            carried = keep.tile([P, width], F32, name=f"carried{m}_{first}")
            picked = res_rows[m][:].indirect(offsets[:, first // 16 : (first + width) // 16])
            nc.vector.tensor_tensor(carried[:], picked, carry[m][:, first : first + width], ALU.mult)
            return carried

        def finish(m, first, width, carried):
            cols = slice(first, first + width)
            result = keep.tile([P, width], F32, name=f"result{m}_{first}")
            nc.vector.tensor_tensor(result[:], carried[:], taken[m][:, cols], ALU.add)
            nc.sync.dma_start(out[m * P : (m + 1) * P, cols], result[:])

        def finish_on_tensor(m, first, width, carried):
            blocks = width // P
            turned = psum.tile([P, blocks, P], F32, name=f"turned{first}")
            for b in range(blocks):
                cols = slice(first + b * P, first + (b + 1) * P)
                nc.tensor.matmul(turned[:, b, :], taken[m][:, cols], identity[:], start=True, stop=False, is_transpose=True)
                nc.tensor.matmul(
                    turned[:, b, :], carried[:, b * P : (b + 1) * P], identity[:], start=False, stop=True, is_transpose=True
                )
            turned_sb = keep.tile([P, blocks, P], F32, name=f"turned_sb{first}")
            nc.scalar.copy(turned_sb[:], turned[:])
            back = psum.tile([P, blocks, P], F32, name=f"back{first}")
            for b in range(blocks):
                nc.tensor.transpose(back[:, b, :], turned_sb[:, b, :], identity[:])
            result = keep.tile([P, width], F32, name=f"result{m}_{first}")
            nc.scalar.copy(result[:], back[:].rearrange("p b c -> p (b c)"))
            nc.scalar.dma_start(out[m * P : (m + 1) * P, first : first + width], result[:])

        layer_share(0, "taken0")
        halves = [res_share(0, h * HALF, HALF) for h in range(2)]
        layer_share(1, "carry0")
        for h in range(2):
            finish_on_tensor(0, h * HALF, HALF, halves[h])
        halves = [res_share(1, h * HALF, HALF) for h in range(2)]
        for h in range(2):
            finish(1, h * HALF, HALF, halves[h])
